import numpy as np
import ml_dtypes


def mxq(x, axis, fmt="e4m3"):
    dtype, down = {"e4m3": (ml_dtypes.float8_e4m3fn, 7), "e5m2": (ml_dtypes.float8_e5m2, 14)}[fmt]
    v = np.moveaxis(np.asarray(x, np.float32).astype(ml_dtypes.bfloat16).astype(np.float64), axis, -1)
    blocks = v.reshape(v.shape[:-1] + (-1, 32))
    amax = np.abs(blocks).max(-1, keepdims=True)
    byte = np.maximum(np.where(amax > 0, np.frexp(amax)[1] - 1 + 127, 0) - down, 1)
    scale = np.exp2(byte - 127.0)
    codes = (blocks / scale).astype(np.float32).astype(dtype).astype(np.float64)
    return np.moveaxis((codes * scale).reshape(v.shape), -1, axis)


WIDE = False


def mx_kscale(k):
    if not WIDE:
        return np.ones(k)
    levels = np.array([10, -10, 5, -5, 0])
    if k % 512:
        return np.exp2(np.random.permutation(np.resize(levels, k // 32))).repeat(32)
    a = np.empty((k // 512, 16))
    for p in range(k // 512):
        a[p, :8] = np.random.permutation(np.resize(levels, 8))
        for g in range(8):
            far = levels[np.abs(levels - a[p, g]) >= 10]
            a[p, g + 8] = far[np.random.randint(len(far))]
    return np.exp2(a.ravel()).repeat(32)


def f64(x):
    return np.asarray(x).astype(np.float64)


def striped(idx):
    return np.tile(idx.reshape(-1, 16).T, (8, 1)).astype(np.uint16)


def unstriped(offs):
    return offs[:16].T.reshape(-1).astype(np.int64)


def pack_weight(w):
    k, n = w.shape
    w = f64(np.asarray(w, np.float32).astype(ml_dtypes.bfloat16)).reshape(k // 32, 32, n)
    amax = np.abs(w).max(1)
    byte = np.clip(np.where(amax > 0, np.frexp(amax)[1] - 1 + 127 - 7, 1), 1, 254)
    scaled = (w * np.exp2(127.0 - byte)[:, None, :]).reshape(k, n).astype(np.float32)
    words = np.ascontiguousarray(scaled.reshape(k // 512, 128, 4, n).transpose(0, 1, 3, 2)).astype(ml_dtypes.float8_e4m3fn).view(np.uint8)
    return words, np.ascontiguousarray(byte.astype(np.uint8).reshape(k // 512, 16, n))


def unpack_weight(words, scales):
    g, p, n, _ = words.shape
    vals = np.ascontiguousarray(words).view(ml_dtypes.float8_e4m3fn).astype(np.float64) * np.repeat(np.exp2(scales.astype(np.float64) - 127.0), 8, axis=1)[..., None]
    return vals.transpose(0, 1, 3, 2).reshape(g * 512, n)


K, T, E, C, N = 512, 4096, 4, 256, 256


def by_expert(wq, xq):
    return np.concatenate([wq[e].T @ xq[:, e * C:(e + 1) * C] for e in range(E)], axis=1)


def setup_inputs():
    n = np.random.standard_normal
    s = mx_kscale(K)[:, None]
    packed = [pack_weight(m) for m in n((E, K, N)) / np.sqrt(K) / s[None]]
    return {
        "xT": (n((K, T)) * s).astype(np.float32),
        "w_words": np.stack([m[0] for m in packed]),
        "w_scales": np.stack([m[1] for m in packed]),
        "gate": np.tile(np.random.uniform(0.2, 1.0, E * C), (N, 1)).astype(np.float32),
        "offs": striped(np.random.permutation(T)[:E * C]),
    }


def reference(xT, w_words, w_scales, gate, offs):
    idx = unstriped(offs)
    xq = mxq(f64(xT)[:, idx], 0, "e4m3")
    w = np.stack([unpack_weight(w_words[e], w_scales[e]) for e in range(E)])
    y = by_expert(w, xq)
    out = np.zeros((N, T))
    out[:, idx] = f64(gate) * y
    return out

@@ -1,0 +1,109 @@
+from contextlib import ExitStack
+
+import concourse.mybir as mybir
+
+K, T, E, C, N = 512, 4096, 4, 256, 256
+FLOPS = 2 * K * N * E * C
+
+F32 = mybir.dt.float32
+BF16 = mybir.dt.bfloat16
+U32 = mybir.dt.uint32
+I32 = mybir.dt.int32
+U16 = mybir.dt.uint16
+U8 = mybir.dt.uint8
+FP8X4 = mybir.dt.float8_e4m3fn_x4
+
+P = 128
+PACK = 4
+SLOTS = E * C
+PIECE = 512
+PIECES = SLOTS // PIECE
+EXPERTS_A_PIECE = PIECE // C
+N_BLOCKS = N // P
+
+
+def tile_routed_moe_kernel(tc, xT, w_words, w_scales, gate, offs, out):
+    nc = tc.nc
+    mult = mybir.AluOpType.mult
+    with ExitStack() as ctx:
+        keep = ctx.enter_context(tc.tile_pool(name="keep", bufs=1))
+        psum = ctx.enter_context(tc.psum_pool(name="psum", bufs=1))
+
+        offsets = keep.tile([P, SLOTS // 16], U16, name="offsets")
+        nc.sync.dma_start(offsets[:], offs)
+
+        x_view = xT.rearrange("(p t) n -> p t n", t=PACK)
+        planes = []
+        for t in range(PACK):
+            plane = keep.tile([P, T], F32, name="plane%d" % t)
+            nc.sync.dma_start(plane[:], x_view[:, t, :])
+            planes.append(plane)
+
+        warm_in = keep.tile([P, 1], F32, name="warm_in")
+        warm_out = keep.tile([P, 1], F32, name="warm_out")
+        nc.vector.memset(warm_in[:], 0.0)
+        nc.scalar.copy(warm_out[:], warm_in[:])
+
+        w_sc = keep.tile([P, E, N], U8, name="w_sc", align_bytes=64)
+        nc.vector.memset(w_sc[:].bitcast(I32), 0)
+        sc_view = w_scales.rearrange("e a (q r) n -> r q (e a) n", r=4)
+        for r in range(4):
+            nc.sync.dma_start(w_sc[r:P:32, :, :].bitcast(I32), sc_view[r].bitcast(I32))
+
+        w_codes = keep.tile([P, E, N], U32, name="w_codes", align_bytes=64)
+        nc.sync.dma_start(
+            w_codes[:].bitcast(I32),
+            w_words.rearrange("e a p n r -> p (e a) (n r)").bitcast(I32),
+        )
+
+        gates = []
+        for b in range(N_BLOCKS):
+            g = keep.tile([P, SLOTS], F32, name="gate%d" % b)
+            nc.sync.dma_start(g[:], gate[b * P:(b + 1) * P, :])
+            gates.append(g)
+
+        windows = []
+        for b in range(N_BLOCKS):
+            w = keep.tile([P, T], F32, name="window%d" % b)
+            nc.vector.memset(w[:], 0.0)
+            windows.append(w)
+
+        sums = [keep.tile([P, SLOTS], F32, name="y%d" % b) for b in range(N_BLOCKS)]
+        for h in range(PIECES):
+            list_h = offsets[:, h * (PIECE // 16):(h + 1) * (PIECE // 16)]
+            grouped = keep.tile([P, PIECE, PACK], BF16, name="grouped%d" % h, align_bytes=64)
+            for t in range(PACK):
+                nc.vector.tensor_copy(grouped[:, :, t], planes[t][:].indirect(list_h))
+            codes = keep.tile([P, PIECE], U32, name="codes%d" % h, align_bytes=64)
+            scales = keep.tile([P, PIECE], U8, name="scales%d" % h, align_bytes=64)
+            nc.vector.quantize_mx(
+                out=codes[:].bitcast(FP8X4),
+                scales=scales[:],
+                in_=grouped[:].rearrange("p c t -> p (c t)"),
+            )
+            for b in range(N_BLOCKS):
+                for i in range(EXPERTS_A_PIECE):
+                    e = h * EXPERTS_A_PIECE + i
+                    acc = psum.tile([P, C], F32, name="acc%d%d" % (e, b))
+                    nc.tensor.matmul_mx(
+                        out=acc[:],
+                        lhsT=w_codes[:, e, b * P:(b + 1) * P].bitcast(FP8X4),
+                        lhsT_scale=w_sc[:, e, b * P:(b + 1) * P],
+                        rhs=codes[:, i * C:(i + 1) * C].bitcast(FP8X4),
+                        rhs_scale=scales[:, i * C:(i + 1) * C],
+                        start=True,
+                        stop=True,
+                    )
+                    nc.scalar.copy(sums[b][:, e * C:(e + 1) * C], acc[:])
+
+        for h in range(PIECES):
+            list_h = offsets[:, h * (PIECE // 16):(h + 1) * (PIECE // 16)]
+            nc.vector.tensor_tensor(
+                windows[0][:].indirect(list_h),
+                sums[0][:, h * PIECE:(h + 1) * PIECE],
+                gates[0][:, h * PIECE:(h + 1) * PIECE],
+                mult,
+            )
+        nc.sync.dma_start(out[0:P, :], windows[0][:])
+        nc.vector.tensor_tensor(windows[1][:].indirect(offsets[:]), sums[1][:], gates[1][:], mult)
+        nc.sync.dma_start(out[P:2 * P, :], windows[1][:])

@@ -30,7 +30,6 @@ def tile_routed_moe_kernel(tc, xT, w_words, w_scales, gate, offs, out):
         psum = ctx.enter_context(tc.psum_pool(name="psum", bufs=1))
 
         offsets = keep.tile([P, SLOTS // 16], U16, name="offsets")
-        nc.sync.dma_start(offsets[:], offs)
 
         x_view = xT.rearrange("(p t) n -> p t n", t=PACK)
         planes = []
@@ -38,6 +37,8 @@ def tile_routed_moe_kernel(tc, xT, w_words, w_scales, gate, offs, out):
             plane = keep.tile([P, T], F32, name="plane%d" % t)
             nc.sync.dma_start(plane[:], x_view[:, t, :])
             planes.append(plane)
+            if t == 0:
+                nc.sync.dma_start(offsets[:], offs)
 
         warm_in = keep.tile([P, 1], F32, name="warm_in")
         warm_out = keep.tile([P, 1], F32, name="warm_out")
@@ -76,11 +77,12 @@ def tile_routed_moe_kernel(tc, xT, w_words, w_scales, gate, offs, out):
                 nc.vector.tensor_copy(grouped[:, :, t], planes[t][:].indirect(list_h))
             codes = keep.tile([P, PIECE], U32, name="codes%d" % h, align_bytes=64)
             scales = keep.tile([P, PIECE], U8, name="scales%d" % h, align_bytes=64)
-            nc.vector.quantize_mx(
-                out=codes[:].bitcast(FP8X4),
-                scales=scales[:],
-                in_=grouped[:].rearrange("p c t -> p (c t)"),
-            )
+            for i in range(EXPERTS_A_PIECE):
+                nc.vector.quantize_mx(
+                    out=codes[:, i * C:(i + 1) * C].bitcast(FP8X4),
+                    scales=scales[:, i * C:(i + 1) * C],
+                    in_=grouped[:, i * C:(i + 1) * C, :].rearrange("p c t -> p (c t)"),
+                )
             for b in range(N_BLOCKS):
                 for i in range(EXPERTS_A_PIECE):
                     e = h * EXPERTS_A_PIECE + i

@@ -70,18 +70,25 @@ def tile_routed_moe_kernel(tc, xT, w_words, w_scales, gate, offs, out):
             windows.append(w)
 
         sums = [keep.tile([P, SLOTS], F32, name="y%d" % b) for b in range(N_BLOCKS)]
-        for h in range(PIECES):
-            list_h = offsets[:, h * (PIECE // 16):(h + 1) * (PIECE // 16)]
-            grouped = keep.tile([P, PIECE, PACK], BF16, name="grouped%d" % h, align_bytes=64)
-            for t in range(PACK):
-                nc.vector.tensor_copy(grouped[:, :, t], planes[t][:].indirect(list_h))
+        lists = [offsets[:, h * (PIECE // 16):(h + 1) * (PIECE // 16)] for h in range(PIECES)]
+        grouped = [keep.tile([P, PIECE, PACK], BF16, name="grouped%d" % h, align_bytes=64) for h in range(PIECES)]
+        for t in range(PACK):
+            for h in range(PIECES):
+                if h == 0 and t >= 2:
+                    dense = keep.tile([P, PIECE], F32, name="dense%d" % t)
+                    nc.vector.tensor_copy(dense[:], planes[t][:].indirect(lists[h]))
+                    nc.scalar.copy(grouped[h][:, :, t], dense[:])
+                else:
+                    nc.vector.tensor_copy(grouped[h][:, :, t], planes[t][:].indirect(lists[h]))
+
+        for h in (1, 0):
             codes = keep.tile([P, PIECE], U32, name="codes%d" % h, align_bytes=64)
             scales = keep.tile([P, PIECE], U8, name="scales%d" % h, align_bytes=64)
             for i in range(EXPERTS_A_PIECE):
                 nc.vector.quantize_mx(
                     out=codes[:, i * C:(i + 1) * C].bitcast(FP8X4),
                     scales=scales[:, i * C:(i + 1) * C],
-                    in_=grouped[:, i * C:(i + 1) * C, :].rearrange("p c t -> p (c t)"),
+                    in_=grouped[h][:, i * C:(i + 1) * C, :].rearrange("p c t -> p (c t)"),
                 )
             for b in range(N_BLOCKS):
                 for i in range(EXPERTS_A_PIECE):
@@ -98,10 +105,9 @@ def tile_routed_moe_kernel(tc, xT, w_words, w_scales, gate, offs, out):
                     )
                     nc.scalar.copy(sums[b][:, e * C:(e + 1) * C], acc[:])
 
-        for h in range(PIECES):
-            list_h = offsets[:, h * (PIECE // 16):(h + 1) * (PIECE // 16)]
+        for h in (1, 0):
             nc.vector.tensor_tensor(
-                windows[0][:].indirect(list_h),
+                windows[0][:].indirect(lists[h]),
                 sums[0][:, h * PIECE:(h + 1) * PIECE],
                 gates[0][:, h * PIECE:(h + 1) * PIECE],
                 mult,

@@ -74,14 +74,15 @@ def tile_routed_moe_kernel(tc, xT, w_words, w_scales, gate, offs, out):
         grouped = [keep.tile([P, PIECE, PACK], BF16, name="grouped%d" % h, align_bytes=64) for h in range(PIECES)]
         for t in range(PACK):
             for h in range(PIECES):
-                if h == 0 and t >= 2:
-                    dense = keep.tile([P, PIECE], F32, name="dense%d" % t)
+                if t >= 2:
+                    dense = keep.tile([P, PIECE], F32, name="dense%d%d" % (h, t))
                     nc.vector.tensor_copy(dense[:], planes[t][:].indirect(lists[h]))
-                    nc.scalar.copy(grouped[h][:, :, t], dense[:])
+                    nc.scalar.copy(grouped[h][:, 0:C, t], dense[:, 0:C])
+                    nc.gpsimd.tensor_copy(grouped[h][:, C:PIECE, t], dense[:, C:PIECE])
                 else:
                     nc.vector.tensor_copy(grouped[h][:, :, t], planes[t][:].indirect(lists[h]))
 
-        for h in (1, 0):
+        for h in range(PIECES):
             codes = keep.tile([P, PIECE], U32, name="codes%d" % h, align_bytes=64)
             scales = keep.tile([P, PIECE], U8, name="scales%d" % h, align_bytes=64)
             for i in range(EXPERTS_A_PIECE):
@@ -105,7 +106,7 @@ def tile_routed_moe_kernel(tc, xT, w_words, w_scales, gate, offs, out):
                     )
                     nc.scalar.copy(sums[b][:, e * C:(e + 1) * C], acc[:])
 
-        for h in (1, 0):
+        for h in range(PIECES):
             nc.vector.tensor_tensor(
                 windows[0][:].indirect(lists[h]),
                 sums[0][:, h * PIECE:(h + 1) * PIECE],

@@ -77,8 +77,12 @@ def tile_routed_moe_kernel(tc, xT, w_words, w_scales, gate, offs, out):
                 if t >= 2:
                     dense = keep.tile([P, PIECE], F32, name="dense%d%d" % (h, t))
                     nc.vector.tensor_copy(dense[:], planes[t][:].indirect(lists[h]))
-                    nc.scalar.copy(grouped[h][:, 0:C, t], dense[:, 0:C])
-                    nc.gpsimd.tensor_copy(grouped[h][:, C:PIECE, t], dense[:, C:PIECE])
+                    share = C // 2 if h == 0 else C
+                    for c0 in range(0, PIECE, 2 * share):
+                        nc.scalar.copy(grouped[h][:, c0:c0 + share, t], dense[:, c0:c0 + share])
+                        nc.gpsimd.tensor_copy(
+                            grouped[h][:, c0 + share:c0 + 2 * share, t], dense[:, c0 + share:c0 + 2 * share]
+                        )
                 else:
                     nc.vector.tensor_copy(grouped[h][:, :, t], planes[t][:].indirect(lists[h]))
 

@@ -77,7 +77,7 @@ def tile_routed_moe_kernel(tc, xT, w_words, w_scales, gate, offs, out):
                 if t >= 2:
                     dense = keep.tile([P, PIECE], F32, name="dense%d%d" % (h, t))
                     nc.vector.tensor_copy(dense[:], planes[t][:].indirect(lists[h]))
-                    share = C // 2 if h == 0 else C
+                    share = C // 2
                     for c0 in range(0, PIECE, 2 * share):
                         nc.scalar.copy(grouped[h][:, c0:c0 + share, t], dense[:, c0:c0 + share])
                         nc.gpsimd.tensor_copy(

from contextlib import ExitStack

import concourse.mybir as mybir

K, T, E, C, N = 512, 4096, 4, 256, 256
FLOPS = 2 * K * N * E * C

F32 = mybir.dt.float32
BF16 = mybir.dt.bfloat16
U32 = mybir.dt.uint32
I32 = mybir.dt.int32
U16 = mybir.dt.uint16
U8 = mybir.dt.uint8
FP8X4 = mybir.dt.float8_e4m3fn_x4

P = 128
PACK = 4
SLOTS = E * C
PIECE = 512
PIECES = SLOTS // PIECE
EXPERTS_A_PIECE = PIECE // C
N_BLOCKS = N // P


def tile_routed_moe_kernel(tc, xT, w_words, w_scales, gate, offs, out):
    nc = tc.nc
    mult = mybir.AluOpType.mult
    with ExitStack() as ctx:
        keep = ctx.enter_context(tc.tile_pool(name="keep", bufs=1))
        psum = ctx.enter_context(tc.psum_pool(name="psum", bufs=1))

        offsets = keep.tile([P, SLOTS // 16], U16, name="offsets")

        x_view = xT.rearrange("(p t) n -> p t n", t=PACK)
        planes = []
        for t in range(PACK):
            plane = keep.tile([P, T], F32, name="plane%d" % t)
            nc.sync.dma_start(plane[:], x_view[:, t, :])
            planes.append(plane)
            if t == 0:
                nc.sync.dma_start(offsets[:], offs)

        warm_in = keep.tile([P, 1], F32, name="warm_in")
        warm_out = keep.tile([P, 1], F32, name="warm_out")
        nc.vector.memset(warm_in[:], 0.0)
        nc.scalar.copy(warm_out[:], warm_in[:])

        w_sc = keep.tile([P, E, N], U8, name="w_sc", align_bytes=64)
        nc.vector.memset(w_sc[:].bitcast(I32), 0)
        sc_view = w_scales.rearrange("e a (q r) n -> r q (e a) n", r=4)
        for r in range(4):
            nc.sync.dma_start(w_sc[r:P:32, :, :].bitcast(I32), sc_view[r].bitcast(I32))

        w_codes = keep.tile([P, E, N], U32, name="w_codes", align_bytes=64)
        nc.sync.dma_start(
            w_codes[:].bitcast(I32),
            w_words.rearrange("e a p n r -> p (e a) (n r)").bitcast(I32),
        )

        gates = []
        for b in range(N_BLOCKS):
            g = keep.tile([P, SLOTS], F32, name="gate%d" % b)
            nc.sync.dma_start(g[:], gate[b * P:(b + 1) * P, :])
            gates.append(g)

        windows = []
        for b in range(N_BLOCKS):
            w = keep.tile([P, T], F32, name="window%d" % b)
            nc.vector.memset(w[:], 0.0)
            windows.append(w)

        sums = [keep.tile([P, SLOTS], F32, name="y%d" % b) for b in range(N_BLOCKS)]
        lists = [offsets[:, h * (PIECE // 16):(h + 1) * (PIECE // 16)] for h in range(PIECES)]
        grouped = [keep.tile([P, PIECE, PACK], BF16, name="grouped%d" % h, align_bytes=64) for h in range(PIECES)]
        for t in range(PACK):
            for h in range(PIECES):
                if t >= 2:
                    dense = keep.tile([P, PIECE], F32, name="dense%d%d" % (h, t))
                    nc.vector.tensor_copy(dense[:], planes[t][:].indirect(lists[h]))
                    share = C // 2
                    for c0 in range(0, PIECE, 2 * share):
                        nc.scalar.copy(grouped[h][:, c0:c0 + share, t], dense[:, c0:c0 + share])
                        nc.gpsimd.tensor_copy(
                            grouped[h][:, c0 + share:c0 + 2 * share, t], dense[:, c0 + share:c0 + 2 * share]
                        )
                else:
                    nc.vector.tensor_copy(grouped[h][:, :, t], planes[t][:].indirect(lists[h]))

        for h in range(PIECES):
            codes = keep.tile([P, PIECE], U32, name="codes%d" % h, align_bytes=64)
            scales = keep.tile([P, PIECE], U8, name="scales%d" % h, align_bytes=64)
            for i in range(EXPERTS_A_PIECE):
                nc.vector.quantize_mx(
                    out=codes[:, i * C:(i + 1) * C].bitcast(FP8X4),
                    scales=scales[:, i * C:(i + 1) * C],
                    in_=grouped[h][:, i * C:(i + 1) * C, :].rearrange("p c t -> p (c t)"),
                )
            for b in range(N_BLOCKS):
                for i in range(EXPERTS_A_PIECE):
                    e = h * EXPERTS_A_PIECE + i
                    acc = psum.tile([P, C], F32, name="acc%d%d" % (e, b))
                    nc.tensor.matmul_mx(
                        out=acc[:],
                        lhsT=w_codes[:, e, b * P:(b + 1) * P].bitcast(FP8X4),
                        lhsT_scale=w_sc[:, e, b * P:(b + 1) * P],
                        rhs=codes[:, i * C:(i + 1) * C].bitcast(FP8X4),
                        rhs_scale=scales[:, i * C:(i + 1) * C],
                        start=True,
                        stop=True,
                    )
                    nc.scalar.copy(sums[b][:, e * C:(e + 1) * C], acc[:])

        for h in range(PIECES):
            nc.vector.tensor_tensor(
                windows[0][:].indirect(lists[h]),
                sums[0][:, h * PIECE:(h + 1) * PIECE],
                gates[0][:, h * PIECE:(h + 1) * PIECE],
                mult,
            )
        nc.sync.dma_start(out[0:P, :], windows[0][:])
        nc.vector.tensor_tensor(windows[1][:].indirect(offsets[:]), sums[1][:], gates[1][:], mult)
        nc.sync.dma_start(out[P:2 * P, :], windows[1][:])
